import numpy as np
import ml_dtypes


def mxq(x, axis, fmt="e4m3"):
    dtype, down = {"e4m3": (ml_dtypes.float8_e4m3fn, 7), "e5m2": (ml_dtypes.float8_e5m2, 14)}[fmt]
    v = np.moveaxis(np.asarray(x, np.float32).astype(ml_dtypes.bfloat16).astype(np.float64), axis, -1)
    blocks = v.reshape(v.shape[:-1] + (-1, 32))
    amax = np.abs(blocks).max(-1, keepdims=True)
    byte = np.maximum(np.where(amax > 0, np.frexp(amax)[1] - 1 + 127, 0) - down, 1)
    scale = np.exp2(byte - 127.0)
    codes = (blocks / scale).astype(np.float32).astype(dtype).astype(np.float64)
    return np.moveaxis((codes * scale).reshape(v.shape), -1, axis)


WIDE = False


def mx_kscale(k):
    if not WIDE:
        return np.ones(k)
    levels = np.array([10, -10, 5, -5, 0])
    if k % 512:
        return np.exp2(np.random.permutation(np.resize(levels, k // 32))).repeat(32)
    a = np.empty((k // 512, 16))
    for p in range(k // 512):
        a[p, :8] = np.random.permutation(np.resize(levels, 8))
        for g in range(8):
            far = levels[np.abs(levels - a[p, g]) >= 10]
            a[p, g + 8] = far[np.random.randint(len(far))]
    return np.exp2(a.ravel()).repeat(32)


def f64(x):
    return np.asarray(x).astype(np.float64)


def striped(idx):
    return np.tile(idx.reshape(-1, 16).T, (8, 1)).astype(np.uint16)


def unstriped(offs):
    return offs[:16].T.reshape(-1).astype(np.int64)


K, T, E, C, N = 512, 2048, 8, 256, 512


def by_expert(wq, xq):
    return np.concatenate([wq[e].T @ xq[:, e * C:(e + 1) * C] for e in range(E)], axis=1)


def setup_inputs():
    n = np.random.standard_normal
    s = mx_kscale(K)[:, None]
    return {
        "xT": (n((K, T)) * s).astype(np.float32),
        "w": (n((E, K, N)) / np.sqrt(K) / s[None]).astype(np.float32),
        "offs": striped(np.random.permutation(T)[:E * C]),
    }


def reference(xT, w, offs):
    idx = unstriped(offs)
    xq = mxq(f64(xT)[:, idx], 0, "e4m3")
    y = by_expert(mxq(f64(w), 1, "e4m3"), xq)
    out = np.zeros((N, T))
    out[:, idx] = y
    return out

@@ -1,0 +1,158 @@
+from contextlib import ExitStack
+
+import concourse.mybir as mybir
+
+K, T, E, C, N = 512, 2048, 8, 256, 512
+FLOPS = 2 * K * N * E * C
+
+F32 = mybir.dt.float32
+BF16 = mybir.dt.bfloat16
+U32 = mybir.dt.uint32
+U16 = mybir.dt.uint16
+U8 = mybir.dt.uint8
+FP8X4 = mybir.dt.float8_e4m3fn_x4
+
+P = 128
+NB = N // P
+X_CUTS = ((0, 512, 1024, 1536, 2048), (0, 512, 1024, 1536, 1792, 2048))
+BANK = 512
+SW = 1024
+UNITS = ((0, 1), (1, 1), (2, 2), (4, 2), (6, 2))
+
+
+def tile_routed_moe_kernel(tc, xT, w, offs, out):
+    nc = tc.nc
+    with ExitStack() as ctx:
+        keep = ctx.enter_context(tc.tile_pool(name="keep", bufs=1))
+        stage = ctx.enter_context(tc.tile_pool(name="stage", bufs=9))
+        wstage = ctx.enter_context(tc.tile_pool(name="wstage", bufs=8))
+        wint = ctx.enter_context(tc.tile_pool(name="wint", bufs=4))
+        psum = ctx.enter_context(tc.psum_pool(name="psum", bufs=8))
+
+        offsets = keep.tile([P, T // 16], U16, name="offsets")
+        nc.sync.dma_start(offsets[:], offs)
+
+        x_view = xT.rearrange("(p j) t -> p j t", j=4)
+        x_raw = {}
+        for u in range(2):
+            for c0, c1 in zip(X_CUTS[u][:-1], X_CUTS[u][1:]):
+                piece = stage.tile([P, 2, c1 - c0], F32, name="xraw_%d_%d" % (u, c0), tag="stage")
+                nc.sync.dma_start(piece[:], x_view[:, 2 * u : 2 * u + 2, c0:c1])
+                x_raw[(u, c0)] = piece
+
+        w_raw = []
+        for e in range(E):
+            raw = wstage.tile([P, 4, N], F32)
+            nc.sync.dma_start(raw[:], w[e].rearrange("(p j) n -> p j n", j=4))
+            w_raw.append(raw)
+
+        x_pairs = []
+        for u in range(2):
+            pairs = keep.tile([P, T, 2], BF16, name="xpairs_%d" % u)
+            x_pairs.append(pairs)
+            for c0, c1 in zip(X_CUTS[u][:-1], X_CUTS[u][1:]):
+                src = x_raw[(u, c0)][:].rearrange("p e t -> p t e")
+                dst = pairs[:, c0:c1, :]
+                if u == 0:
+                    nc.vector.tensor_copy(out=dst, in_=src)
+                else:
+                    nc.scalar.copy(out=dst, in_=src)
+
+        widths = [n * C for (first, n) in UNITS]
+        starts = [first * C for (first, n) in UNITS]
+        n_units = len(UNITS)
+        x_words = [keep.tile([P, 4 * widths[k]], BF16, name="xw_%d" % k) for k in range(n_units)]
+        x_grouped = [keep.tile([P, 4 * widths[k]], BF16, name="xg_%d" % k, align_bytes=64) for k in range(n_units)]
+        x_codes = [keep.tile([P, widths[k]], U32, name="xc_%d" % k, align_bytes=64) for k in range(n_units)]
+        x_scales = [keep.tile([P, widths[k]], U8, name="xs_%d" % k, align_bytes=64) for k in range(n_units)]
+        sums = {}
+        for k in range(n_units):
+            for i in range(NB * widths[k] // SW):
+                sums[(k, i)] = stage.tile([P, SW], F32, name="sums_%d_%d" % (k, i), tag="stage")
+        windows = [keep.tile([P, T], F32, name="window_%d" % b) for b in range(NB)]
+        w_codes = {}
+        w_scales = {}
+        banks = {}
+
+        def unit_offsets(k):
+            return offsets[:, starts[k] // 16 : (starts[k] + widths[k]) // 16]
+
+        def gather(u, k):
+            table = x_pairs[u][:].rearrange("p t e -> p (t e)").bitcast(U32)
+            nc.vector.tensor_copy(
+                out=x_words[k][:].bitcast(U32)[:, u * widths[k] : (u + 1) * widths[k]],
+                in_=table.indirect(unit_offsets(k)),
+            )
+
+        def prepare(k):
+            nc.scalar.copy(
+                out=x_grouped[k][:].rearrange("p (s u e) -> p s u e", u=2, e=2),
+                in_=x_words[k][:].rearrange("p (u s e) -> p s u e", u=2, e=2),
+            )
+            nc.vector.quantize_mx(
+                out=x_codes[k][:].bitcast(FP8X4), scales=x_scales[k][:], in_=x_grouped[k][:]
+            )
+            first, n = UNITS[k]
+            cols = N // 2 if k == 0 else N
+            for i in range(NB * widths[k] // BANK):
+                banks[(k, i)] = psum.tile([P, BANK], F32, name="acc", tag="acc")
+            for n0 in range(0, N, cols):
+              for e in range(first, first + n):
+                grouped = wint.tile([P, cols, 4], BF16, align_bytes=64)
+                nc.scalar.copy(
+                    out=grouped[:].rearrange("p (c i) j -> p c j i", i=4),
+                    in_=w_raw[e][:, :, n0 : n0 + cols].rearrange("p j (c i) -> p c j i", i=4),
+                )
+                codes = keep.tile([P, cols], U32, name="wc_%d_%d" % (e, n0), align_bytes=64)
+                scales = keep.tile([P, cols], U8, name="ws_%d_%d" % (e, n0), align_bytes=64)
+                nc.vector.quantize_mx(
+                    out=codes[:].bitcast(FP8X4),
+                    scales=scales[:],
+                    in_=grouped[:].rearrange("p n j -> p (n j)"),
+                )
+                w_codes[e] = codes
+                w_scales[e] = scales
+              for b in range(n0 // P, (n0 + cols) // P):
+                for e in range(first, first + n):
+                    s = (e - first) * C
+                    flat = b * widths[k] + s
+                    m0 = b * P - n0
+                    nc.tensor.matmul_mx(
+                        out=banks[(k, flat // BANK)][:, flat % BANK : flat % BANK + C],
+                        lhsT=w_codes[e][:, m0 : m0 + P].bitcast(FP8X4),
+                        lhsT_scale=w_scales[e][:, m0 : m0 + P],
+                        rhs=x_codes[k][:, s : s + C].bitcast(FP8X4),
+                        rhs_scale=x_scales[k][:, s : s + C],
+                        start=True,
+                        stop=True,
+                    )
+
+        def send_back(k, blocks):
+            lo = blocks[0] * widths[k]
+            hi = (blocks[-1] + 1) * widths[k]
+            for flat in range(lo, hi, BANK):
+                nc.scalar.copy(
+                    out=sums[(k, flat // SW)][:, flat % SW : flat % SW + BANK],
+                    in_=banks[(k, flat // BANK)][:],
+                )
+            for b in blocks:
+                flat = b * widths[k]
+                nc.vector.tensor_copy(
+                    out=windows[b][:].indirect(unit_offsets(k)),
+                    in_=sums[(k, flat // SW)][:, flat % SW : flat % SW + widths[k]],
+                )
+                if k == n_units - 1:
+                    nc.sync.dma_start(out[b * P : (b + 1) * P, :], windows[b][:])
+
+        for k in range(n_units):
+            gather(0, k)
+        gather(1, 0)
+        gather(1, 1)
+        prepare(0)
+        for k in range(2, n_units):
+            gather(1, k)
+        for k in range(n_units):
+            send_back(k, (0, 1))
+            if k + 1 < n_units:
+                prepare(k + 1)
+            send_back(k, (2, 3))

@@ -11,10 +11,12 @@ U32 = mybir.dt.uint32
 U16 = mybir.dt.uint16
 U8 = mybir.dt.uint8
 FP8X4 = mybir.dt.float8_e4m3fn_x4
+COPY = mybir.ActivationFunctionType.Copy
 
 P = 128
 NB = N // P
-X_CUTS = ((0, 512, 1024, 1536, 2048), (0, 512, 1024, 1536, 1792, 2048))
+PAIR_CUTS = (0, 512, 1024, 1536, 2048)
+PLANE_CUTS = {2: (0, 1024, 2048), 3: (0, 1024, 1536, 2048)}
 BANK = 512
 SW = 1024
 UNITS = ((0, 1), (1, 1), (2, 2), (4, 2), (6, 2))
@@ -33,35 +35,40 @@ def tile_routed_moe_kernel(tc, xT, w, offs, out):
         nc.sync.dma_start(offsets[:], offs)
 
         x_view = xT.rearrange("(p j) t -> p j t", j=4)
-        x_raw = {}
-        for u in range(2):
-            for c0, c1 in zip(X_CUTS[u][:-1], X_CUTS[u][1:]):
-                piece = stage.tile([P, 2, c1 - c0], F32, name="xraw_%d_%d" % (u, c0), tag="stage")
-                nc.sync.dma_start(piece[:], x_view[:, 2 * u : 2 * u + 2, c0:c1])
-                x_raw[(u, c0)] = piece
+        pair_raw = {}
+        for c0, c1 in zip(PAIR_CUTS[:-1], PAIR_CUTS[1:]):
+            piece = stage.tile([P, 2, c1 - c0], F32, name="xpair_%d" % c0, tag="stage")
+            nc.sync.dma_start(piece[:], x_view[:, 0:2, c0:c1])
+            pair_raw[c0] = piece
+        plane_raw = {}
+        for j in (2, 3):
+            for c0, c1 in zip(PLANE_CUTS[j][:-1], PLANE_CUTS[j][1:]):
+                piece = stage.tile([P, c1 - c0], F32, name="xplane_%d_%d" % (j, c0), tag="stage")
+                nc.sync.dma_start(piece[:], x_view[:, j, c0:c1])
+                plane_raw[(j, c0)] = piece
 
         w_raw = []
         for e in range(E):
             raw = wstage.tile([P, 4, N], F32)
-            nc.sync.dma_start(raw[:], w[e].rearrange("(p j) n -> p j n", j=4))
+            w_view = w[e].rearrange("(p j) n -> p j n", j=4)
+            if e == 0:
+                nc.sync.dma_start(raw[:, :, 0 : N // 2], w_view[:, :, 0 : N // 2])
+                nc.sync.dma_start(raw[:, :, N // 2 : N], w_view[:, :, N // 2 : N])
+            else:
+                nc.sync.dma_start(raw[:], w_view)
             w_raw.append(raw)
 
-        x_pairs = []
-        for u in range(2):
-            pairs = keep.tile([P, T, 2], BF16, name="xpairs_%d" % u)
-            x_pairs.append(pairs)
-            for c0, c1 in zip(X_CUTS[u][:-1], X_CUTS[u][1:]):
-                src = x_raw[(u, c0)][:].rearrange("p e t -> p t e")
-                dst = pairs[:, c0:c1, :]
-                if u == 0:
-                    nc.vector.tensor_copy(out=dst, in_=src)
-                else:
-                    nc.scalar.copy(out=dst, in_=src)
+        pairs = keep.tile([P, T, 2], BF16, name="xpairs")
+        for c0, c1 in zip(PAIR_CUTS[:-1], PAIR_CUTS[1:]):
+            nc.vector.tensor_copy(out=pairs[:, c0:c1, :], in_=pair_raw[c0][:].rearrange("p e t -> p t e"))
+        planes = keep.tile([P, 2, T], BF16, name="xplanes")
+        for j in (2, 3):
+            for c0, c1 in zip(PLANE_CUTS[j][:-1], PLANE_CUTS[j][1:]):
+                nc.scalar.copy(out=planes[:, j - 2, c0:c1], in_=plane_raw[(j, c0)][:])
 
         widths = [n * C for (first, n) in UNITS]
         starts = [first * C for (first, n) in UNITS]
         n_units = len(UNITS)
-        x_words = [keep.tile([P, 4 * widths[k]], BF16, name="xw_%d" % k) for k in range(n_units)]
         x_grouped = [keep.tile([P, 4 * widths[k]], BF16, name="xg_%d" % k, align_bytes=64) for k in range(n_units)]
         x_codes = [keep.tile([P, widths[k]], U32, name="xc_%d" % k, align_bytes=64) for k in range(n_units)]
         x_scales = [keep.tile([P, widths[k]], U8, name="xs_%d" % k, align_bytes=64) for k in range(n_units)]
@@ -77,18 +84,22 @@ def tile_routed_moe_kernel(tc, xT, w, offs, out):
         def unit_offsets(k):
             return offsets[:, starts[k] // 16 : (starts[k] + widths[k]) // 16]
 
-        def gather(u, k):
-            table = x_pairs[u][:].rearrange("p t e -> p (t e)").bitcast(U32)
+        def gather_pairs(k):
+            table = pairs[:].rearrange("p t e -> p (t e)").bitcast(U32)
             nc.vector.tensor_copy(
-                out=x_words[k][:].bitcast(U32)[:, u * widths[k] : (u + 1) * widths[k]],
+                out=x_grouped[k][:].bitcast(U32).rearrange("p (s u) -> p s u", u=2)[:, :, 0],
                 in_=table.indirect(unit_offsets(k)),
             )
 
+        def gather_planes(k):
+            for j in (2, 3):
+                nc.scalar.activation(
+                    out=x_grouped[k][:].rearrange("p (s j) -> p s j", j=4)[:, :, j],
+                    in_=planes[:, j - 2, :].indirect(unit_offsets(k)),
+                    func=COPY,
+                )
+
         def prepare(k):
-            nc.scalar.copy(
-                out=x_grouped[k][:].rearrange("p (s u e) -> p s u e", u=2, e=2),
-                in_=x_words[k][:].rearrange("p (u s e) -> p s u e", u=2, e=2),
-            )
             nc.vector.quantize_mx(
                 out=x_codes[k][:].bitcast(FP8X4), scales=x_scales[k][:], in_=x_grouped[k][:]
             )
@@ -99,10 +110,12 @@ def tile_routed_moe_kernel(tc, xT, w, offs, out):
             for n0 in range(0, N, cols):
               for e in range(first, first + n):
                 grouped = wint.tile([P, cols, 4], BF16, align_bytes=64)
-                nc.scalar.copy(
-                    out=grouped[:].rearrange("p (c i) j -> p c j i", i=4),
-                    in_=w_raw[e][:, :, n0 : n0 + cols].rearrange("p j (c i) -> p c j i", i=4),
-                )
+                dst = grouped[:].rearrange("p (c i) j -> p c j i", i=4)
+                src = w_raw[e][:, :, n0 : n0 + cols].rearrange("p j (c i) -> p c j i", i=4)
+                if k == 0 and n0 == 0:
+                    nc.vector.tensor_copy(out=dst, in_=src)
+                else:
+                    nc.scalar.copy(out=dst, in_=src)
                 codes = keep.tile([P, cols], U32, name="wc_%d_%d" % (e, n0), align_bytes=64)
                 scales = keep.tile([P, cols], U8, name="ws_%d_%d" % (e, n0), align_bytes=64)
                 nc.vector.quantize_mx(
@@ -145,14 +158,15 @@ def tile_routed_moe_kernel(tc, xT, w, offs, out):
                     nc.sync.dma_start(out[b * P : (b + 1) * P, :], windows[b][:])
 
         for k in range(n_units):
-            gather(0, k)
-        gather(1, 0)
-        gather(1, 1)
+            gather_pairs(k)
+        gather_planes(0)
         prepare(0)
-        for k in range(2, n_units):
-            gather(1, k)
         for k in range(n_units):
             send_back(k, (0, 1))
+            if k == 0:
+                gather_planes(1)
             if k + 1 < n_units:
                 prepare(k + 1)
             send_back(k, (2, 3))
+            if k + 2 < n_units:
+                gather_planes(k + 2)

@@ -143,11 +143,14 @@ def tile_routed_moe_kernel(tc, xT, w, offs, out):
         def send_back(k, blocks):
             lo = blocks[0] * widths[k]
             hi = (blocks[-1] + 1) * widths[k]
-            for flat in range(lo, hi, BANK):
-                nc.scalar.copy(
-                    out=sums[(k, flat // SW)][:, flat % SW : flat % SW + BANK],
-                    in_=banks[(k, flat // BANK)][:],
-                )
+            step = C if k == 0 else BANK
+            for flat in range(lo, hi, step):
+                dst = sums[(k, flat // SW)][:, flat % SW : flat % SW + step]
+                src = banks[(k, flat // BANK)][:, flat % BANK : flat % BANK + step]
+                if k == 0 and flat == 0:
+                    nc.vector.tensor_copy(out=dst, in_=src)
+                else:
+                    nc.scalar.copy(out=dst, in_=src)
             for b in blocks:
                 flat = b * widths[k]
                 nc.vector.tensor_copy(

@@ -15,67 +15,65 @@ COPY = mybir.ActivationFunctionType.Copy
 
 P = 128
 NB = N // P
-PAIR_CUTS = (0, 512, 1024, 1536, 2048)
-PLANE_CUTS = {2: (0, 1024, 2048), 3: (0, 1024, 1536, 2048)}
+PIECES = ((0, 1024), (1024, 1536), (1536, 2048))
+LAST = 1792
+CASTS = ((2, 0, 1024, "scalar"), (2, 1024, LAST, "scalar"), (3, 0, 512, "vector"), (3, 512, 1024, "vector"), (3, 1024, LAST, "scalar"))
 BANK = 512
 SW = 1024
-UNITS = ((0, 1), (1, 1), (2, 2), (4, 2), (6, 2))
+UNITS = ((0, 1), (1, 1), (2, 1), (3, 1), (4, 2), (6, 2))
+WCUT = 256
+W0_CUTS = (0, 128, 256, 512)
 
 
 def tile_routed_moe_kernel(tc, xT, w, offs, out):
     nc = tc.nc
     with ExitStack() as ctx:
         keep = ctx.enter_context(tc.tile_pool(name="keep", bufs=1))
-        stage = ctx.enter_context(tc.tile_pool(name="stage", bufs=9))
+        stage = ctx.enter_context(tc.tile_pool(name="stage", bufs=3))
+        sums_pool = ctx.enter_context(tc.tile_pool(name="sums", bufs=4))
         wstage = ctx.enter_context(tc.tile_pool(name="wstage", bufs=8))
         wint = ctx.enter_context(tc.tile_pool(name="wint", bufs=4))
         psum = ctx.enter_context(tc.psum_pool(name="psum", bufs=8))
 
-        offsets = keep.tile([P, T // 16], U16, name="offsets")
-        nc.sync.dma_start(offsets[:], offs)
-
         x_view = xT.rearrange("(p j) t -> p j t", j=4)
-        pair_raw = {}
-        for c0, c1 in zip(PAIR_CUTS[:-1], PAIR_CUTS[1:]):
+        pair_raw = []
+        for c0, c1 in PIECES:
             piece = stage.tile([P, 2, c1 - c0], F32, name="xpair_%d" % c0, tag="stage")
             nc.sync.dma_start(piece[:], x_view[:, 0:2, c0:c1])
-            pair_raw[c0] = piece
-        plane_raw = {}
-        for j in (2, 3):
-            for c0, c1 in zip(PLANE_CUTS[j][:-1], PLANE_CUTS[j][1:]):
-                piece = stage.tile([P, c1 - c0], F32, name="xplane_%d_%d" % (j, c0), tag="stage")
-                nc.sync.dma_start(piece[:], x_view[:, j, c0:c1])
-                plane_raw[(j, c0)] = piece
+            pair_raw.append(piece)
+        offsets = keep.tile([P, T // 16], U16, name="offsets")
+        nc.sync.dma_start(offsets[:], offs)
+        w_raw = [wstage.tile([P, 4, N], F32, name="w_raw_%d" % e, tag="w_raw") for e in range(E)]
+        raw23 = keep.tile([P, 2, T], F32, name="raw23")
+        plane_raw = {j: raw23[:, j - 2, :] for j in (2, 3)}
 
-        w_raw = []
-        for e in range(E):
-            raw = wstage.tile([P, 4, N], F32)
-            w_view = w[e].rearrange("(p j) n -> p j n", j=4)
-            if e == 0:
-                nc.sync.dma_start(raw[:, :, 0 : N // 2], w_view[:, :, 0 : N // 2])
-                nc.sync.dma_start(raw[:, :, N // 2 : N], w_view[:, :, N // 2 : N])
-            else:
-                nc.sync.dma_start(raw[:], w_view)
-            w_raw.append(raw)
+        def load_w(e, n0, n1):
+            nc.sync.dma_start(w_raw[e][:, :, n0:n1], w[e].rearrange("(p j) n -> p j n", j=4)[:, :, n0:n1])
+
+        nc.sync.dma_start(plane_raw[2], x_view[:, 2, :])
+        load_w(0, W0_CUTS[0], W0_CUTS[1])
+        nc.sync.dma_start(plane_raw[3], x_view[:, 3, :])
+        for n0, n1 in zip(W0_CUTS[1:-1], W0_CUTS[2:]):
+            load_w(0, n0, n1)
+        for e in range(1, E):
+            load_w(e, 0, N)
 
         pairs = keep.tile([P, T, 2], BF16, name="xpairs")
-        for c0, c1 in zip(PAIR_CUTS[:-1], PAIR_CUTS[1:]):
-            nc.vector.tensor_copy(out=pairs[:, c0:c1, :], in_=pair_raw[c0][:].rearrange("p e t -> p t e"))
-        planes = keep.tile([P, 2, T], BF16, name="xplanes")
-        for j in (2, 3):
-            for c0, c1 in zip(PLANE_CUTS[j][:-1], PLANE_CUTS[j][1:]):
-                nc.scalar.copy(out=planes[:, j - 2, c0:c1], in_=plane_raw[(j, c0)][:])
+        planes = keep.tile([P, 4, T], BF16, name="xplanes")
+        for (c0, c1), piece in zip(PIECES, pair_raw):
+            nc.vector.tensor_copy(out=pairs[:, c0:c1, :], in_=piece[:].rearrange("p e t -> p t e"))
+            nc.scalar.copy(out=planes[:, 0:2, c0:c1], in_=piece[:])
 
         widths = [n * C for (first, n) in UNITS]
         starts = [first * C for (first, n) in UNITS]
         n_units = len(UNITS)
-        x_grouped = [keep.tile([P, 4 * widths[k]], BF16, name="xg_%d" % k, align_bytes=64) for k in range(n_units)]
+        x_grouped = {}
+        for k in range(n_units - 2):
+            tag = "xg_last" if k == 2 else "xg_%d" % k
+            x_grouped[k] = keep.tile([P, 4 * widths[k]], BF16, name="xg_%d" % k, tag=tag, align_bytes=64)
         x_codes = [keep.tile([P, widths[k]], U32, name="xc_%d" % k, align_bytes=64) for k in range(n_units)]
         x_scales = [keep.tile([P, widths[k]], U8, name="xs_%d" % k, align_bytes=64) for k in range(n_units)]
         sums = {}
-        for k in range(n_units):
-            for i in range(NB * widths[k] // SW):
-                sums[(k, i)] = stage.tile([P, SW], F32, name="sums_%d_%d" % (k, i), tag="stage")
         windows = [keep.tile([P, T], F32, name="window_%d" % b) for b in range(NB)]
         w_codes = {}
         w_scales = {}
@@ -84,92 +82,129 @@ def tile_routed_moe_kernel(tc, xT, w, offs, out):
         def unit_offsets(k):
             return offsets[:, starts[k] // 16 : (starts[k] + widths[k]) // 16]
 
-        def gather_pairs(k):
+        def slot_planes(k):
+            return x_grouped[k][:].rearrange("p (s j) -> p s j", j=4)
+
+        def gather_words(k):
             table = pairs[:].rearrange("p t e -> p (t e)").bitcast(U32)
             nc.vector.tensor_copy(
                 out=x_grouped[k][:].bitcast(U32).rearrange("p (s u) -> p s u", u=2)[:, :, 0],
                 in_=table.indirect(unit_offsets(k)),
             )
 
-        def gather_planes(k):
-            for j in (2, 3):
+        def gather_raw(k, j):
+            nc.vector.tensor_copy(out=slot_planes(k)[:, :, j], in_=plane_raw[j].indirect(unit_offsets(k)))
+
+        def gather_planes(k, which):
+            for j in which:
                 nc.scalar.activation(
-                    out=x_grouped[k][:].rearrange("p (s j) -> p s j", j=4)[:, :, j],
-                    in_=planes[:, j - 2, :].indirect(unit_offsets(k)),
-                    func=COPY,
+                    out=slot_planes(k)[:, :, j], in_=planes[:, j, :].indirect(unit_offsets(k)), func=COPY
                 )
+
+        def gather_late(k):
+            if k >= n_units - 2:
+                x_grouped[k] = keep.tile([P, 4 * widths[k]], BF16, name="xg_late_%d" % k, tag="xg_last", align_bytes=64)
+            gather_planes(k, (0, 1, 2, 3) if k >= n_units - 2 else (2, 3))
+
+        def quantize_x(k):
+            nc.vector.quantize_mx(out=x_codes[k][:].bitcast(FP8X4), scales=x_scales[k][:], in_=x_grouped[k][:])
+
+        def interleave(e, n0, n1, copy):
+            grouped = wint.tile([P, n1 - n0, 4], BF16, align_bytes=64)
+            copy(
+                out=grouped[:].rearrange("p (c i) j -> p c j i", i=4),
+                in_=w_raw[e][:, :, n0:n1].rearrange("p j (c i) -> p c j i", i=4),
+            )
+            return grouped
+
+        def quantize_w(e, n0, n1, grouped):
+            codes = keep.tile([P, n1 - n0], U32, name="wc_%d_%d" % (e, n0), align_bytes=64)
+            scales = keep.tile([P, n1 - n0], U8, name="ws_%d_%d" % (e, n0), align_bytes=64)
+            nc.vector.quantize_mx(
+                out=codes[:].bitcast(FP8X4), scales=scales[:], in_=grouped[:].rearrange("p n j -> p (n j)")
+            )
+            for b in range(n0 // P, n1 // P):
+                w_codes[(e, b)] = codes[:, b * P - n0 : (b + 1) * P - n0]
+                w_scales[(e, b)] = scales[:, b * P - n0 : (b + 1) * P - n0]
+
+        def multiply(k, e, b, acc):
+            s = (e - UNITS[k][0]) * C
+            nc.tensor.matmul_mx(
+                out=acc,
+                lhsT=w_codes[(e, b)].bitcast(FP8X4),
+                lhsT_scale=w_scales[(e, b)],
+                rhs=x_codes[k][:, s : s + C].bitcast(FP8X4),
+                rhs_scale=x_scales[k][:, s : s + C],
+                start=True,
+                stop=True,
+            )
+
+        def scatter(k, b):
+            flat = b * widths[k]
+            nc.vector.tensor_copy(
+                out=windows[b][:].indirect(unit_offsets(k)),
+                in_=sums[(k, flat // SW)][:, flat % SW : flat % SW + widths[k]],
+            )
 
         def prepare(k):
-            nc.vector.quantize_mx(
-                out=x_codes[k][:].bitcast(FP8X4), scales=x_scales[k][:], in_=x_grouped[k][:]
-            )
             first, n = UNITS[k]
-            cols = N // 2 if k == 0 else N
+            quantize_x(k)
             for i in range(NB * widths[k] // BANK):
                 banks[(k, i)] = psum.tile([P, BANK], F32, name="acc", tag="acc")
-            for n0 in range(0, N, cols):
-              for e in range(first, first + n):
-                grouped = wint.tile([P, cols, 4], BF16, align_bytes=64)
-                dst = grouped[:].rearrange("p (c i) j -> p c j i", i=4)
-                src = w_raw[e][:, :, n0 : n0 + cols].rearrange("p j (c i) -> p c j i", i=4)
-                if k == 0 and n0 == 0:
-                    nc.vector.tensor_copy(out=dst, in_=src)
-                else:
-                    nc.scalar.copy(out=dst, in_=src)
-                codes = keep.tile([P, cols], U32, name="wc_%d_%d" % (e, n0), align_bytes=64)
-                scales = keep.tile([P, cols], U8, name="ws_%d_%d" % (e, n0), align_bytes=64)
-                nc.vector.quantize_mx(
-                    out=codes[:].bitcast(FP8X4),
-                    scales=scales[:],
-                    in_=grouped[:].rearrange("p n j -> p (n j)"),
-                )
-                w_codes[e] = codes
-                w_scales[e] = scales
-              for b in range(n0 // P, (n0 + cols) // P):
+            for n0 in range(0, N, WCUT):
                 for e in range(first, first + n):
-                    s = (e - first) * C
-                    flat = b * widths[k] + s
-                    m0 = b * P - n0
-                    nc.tensor.matmul_mx(
-                        out=banks[(k, flat // BANK)][:, flat % BANK : flat % BANK + C],
-                        lhsT=w_codes[e][:, m0 : m0 + P].bitcast(FP8X4),
-                        lhsT_scale=w_scales[e][:, m0 : m0 + P],
-                        rhs=x_codes[k][:, s : s + C].bitcast(FP8X4),
-                        rhs_scale=x_scales[k][:, s : s + C],
-                        start=True,
-                        stop=True,
-                    )
+                    quantize_w(e, n0, n0 + WCUT, interleave(e, n0, n0 + WCUT, nc.scalar.copy))
+                for b in range(n0 // P, (n0 + WCUT) // P):
+                    for e in range(first, first + n):
+                        flat = b * widths[k] + (e - first) * C
+                        multiply(k, e, b, banks[(k, flat // BANK)][:, flat % BANK : flat % BANK + C])
 
         def send_back(k, blocks):
-            lo = blocks[0] * widths[k]
-            hi = (blocks[-1] + 1) * widths[k]
-            step = C if k == 0 else BANK
-            for flat in range(lo, hi, step):
-                dst = sums[(k, flat // SW)][:, flat % SW : flat % SW + step]
-                src = banks[(k, flat // BANK)][:, flat % BANK : flat % BANK + step]
-                if k == 0 and flat == 0:
-                    nc.vector.tensor_copy(out=dst, in_=src)
-                else:
-                    nc.scalar.copy(out=dst, in_=src)
-            for b in blocks:
-                flat = b * widths[k]
-                nc.vector.tensor_copy(
-                    out=windows[b][:].indirect(unit_offsets(k)),
-                    in_=sums[(k, flat // SW)][:, flat % SW : flat % SW + widths[k]],
+            step = min(widths[k], BANK)
+            for flat in range(blocks[0] * widths[k], (blocks[-1] + 1) * widths[k], step):
+                if flat % SW == 0:
+                    sums[(k, flat // SW)] = sums_pool.tile([P, SW], F32, name="sums_%d_%d" % (k, flat // SW), tag="sums")
+                nc.scalar.copy(
+                    out=sums[(k, flat // SW)][:, flat % SW : flat % SW + step],
+                    in_=banks[(k, flat // BANK)][:, flat % BANK : flat % BANK + step],
                 )
+            for b in blocks:
+                scatter(k, b)
                 if k == n_units - 1:
                     nc.sync.dma_start(out[b * P : (b + 1) * P, :], windows[b][:])
 
-        for k in range(n_units):
-            gather_pairs(k)
-        gather_planes(0)
-        prepare(0)
-        for k in range(n_units):
+        for k in range(n_units - 2):
+            gather_words(k)
+        gather_raw(0, 2)
+        gather_raw(0, 3)
+        sums[(0, 0)] = sums_pool.tile([P, SW], F32, name="sums_0_0", tag="sums")
+        acc0 = [psum.tile([P, BANK], F32, name="acc0_%d" % b, tag="acc") for b in range(NB)]
+        for n0, n1 in zip(W0_CUTS[:-1], W0_CUTS[1:]):
+            first_cut = n0 == 0
+            grouped = interleave(0, n0, n1, nc.vector.tensor_copy if first_cut else nc.scalar.copy)
+            if first_cut:
+                quantize_x(0)
+            quantize_w(0, n0, n1, grouped)
+            for b in range(n0 // P, n1 // P):
+                multiply(0, 0, b, acc0[b][:, 0:C])
+            for b in range(n0 // P, n1 // P):
+                copy = nc.vector.tensor_copy if b == 0 else nc.scalar.copy
+                copy(out=sums[(0, 0)][:, b * C : (b + 1) * C], in_=acc0[b][:, 0:C])
+                scatter(0, b)
+        for j, c0, c1, copy in CASTS:
+            engine = nc.vector.tensor_copy if copy == "vector" else nc.scalar.copy
+            engine(out=planes[:, j, c0:c1], in_=plane_raw[j][:, c0:c1])
+        nc.scalar.copy(out=planes[:, 2:4, LAST:T], in_=raw23[:, :, LAST:T])
+
+        gather_planes(1, (2, 3))
+        prepare(1)
+        gather_planes(2, (2, 3))
+        for k in range(1, n_units):
             send_back(k, (0, 1))
-            if k == 0:
-                gather_planes(1)
+            if k + 1 == n_units - 1:
+                gather_late(k + 1)
             if k + 1 < n_units:
                 prepare(k + 1)
             send_back(k, (2, 3))
-            if k + 2 < n_units:
-                gather_planes(k + 2)
+            if k + 2 < n_units - 1:
+                gather_late(k + 2)

@@ -21,7 +21,11 @@ CASTS = ((2, 0, 1024, "scalar"), (2, 1024, LAST, "scalar"), (3, 0, 512, "vector"
 BANK = 512
 SW = 1024
 UNITS = ((0, 1), (1, 1), (2, 1), (3, 1), (4, 2), (6, 2))
-WCUT = 256
+WORDS = (0, 1, 2, 3)
+EXTRA = {1: ((4, 0), (4, 1)), 2: ((5, 0),), 3: ((5, 1),)}
+LATE0 = True
+SPLIT = 2
+VIL = ((1, 0),)
 W0_CUTS = (0, 128, 256, 512)
 
 
@@ -69,8 +73,7 @@ def tile_routed_moe_kernel(tc, xT, w, offs, out):
         n_units = len(UNITS)
         x_grouped = {}
         for k in range(n_units - 2):
-            tag = "xg_last" if k == 2 else "xg_%d" % k
-            x_grouped[k] = keep.tile([P, 4 * widths[k]], BF16, name="xg_%d" % k, tag=tag, align_bytes=64)
+            x_grouped[k] = keep.tile([P, 4 * widths[k]], BF16, name="xg_%d" % k, tag="xg_%d" % k, align_bytes=64)
         x_codes = [keep.tile([P, widths[k]], U32, name="xc_%d" % k, align_bytes=64) for k in range(n_units)]
         x_scales = [keep.tile([P, widths[k]], U8, name="xs_%d" % k, align_bytes=64) for k in range(n_units)]
         sums = {}
@@ -102,9 +105,7 @@ def tile_routed_moe_kernel(tc, xT, w, offs, out):
                 )
 
         def gather_late(k):
-            if k >= n_units - 2:
-                x_grouped[k] = keep.tile([P, 4 * widths[k]], BF16, name="xg_late_%d" % k, tag="xg_last", align_bytes=64)
-            gather_planes(k, (0, 1, 2, 3) if k >= n_units - 2 else (2, 3))
+            gather_planes(k, (2, 3))
 
         def quantize_x(k):
             nc.vector.quantize_mx(out=x_codes[k][:].bitcast(FP8X4), scales=x_scales[k][:], in_=x_grouped[k][:])
@@ -146,23 +147,25 @@ def tile_routed_moe_kernel(tc, xT, w, offs, out):
                 in_=sums[(k, flat // SW)][:, flat % SW : flat % SW + widths[k]],
             )
 
-        def prepare(k):
-            first, n = UNITS[k]
+        def open_banks(k):
             quantize_x(k)
             for i in range(NB * widths[k] // BANK):
                 banks[(k, i)] = psum.tile([P, BANK], F32, name="acc", tag="acc")
-            for n0 in range(0, N, WCUT):
+
+        def weights(k, n0, n1):
+            first, n = UNITS[k]
+            for e in range(first, first + n):
+                copy = nc.vector.tensor_copy if (e, n0) in VIL else nc.scalar.copy
+                quantize_w(e, n0, n1, interleave(e, n0, n1, copy))
+            for b in range(n0 // P, n1 // P):
                 for e in range(first, first + n):
-                    quantize_w(e, n0, n0 + WCUT, interleave(e, n0, n0 + WCUT, nc.scalar.copy))
-                for b in range(n0 // P, (n0 + WCUT) // P):
-                    for e in range(first, first + n):
-                        flat = b * widths[k] + (e - first) * C
-                        multiply(k, e, b, banks[(k, flat // BANK)][:, flat % BANK : flat % BANK + C])
+                    flat = b * widths[k] + (e - first) * C
+                    multiply(k, e, b, banks[(k, flat // BANK)][:, flat % BANK : flat % BANK + C])
 
         def send_back(k, blocks):
             step = min(widths[k], BANK)
             for flat in range(blocks[0] * widths[k], (blocks[-1] + 1) * widths[k], step):
-                if flat % SW == 0:
+                if (k, flat // SW) not in sums:
                     sums[(k, flat // SW)] = sums_pool.tile([P, SW], F32, name="sums_%d_%d" % (k, flat // SW), tag="sums")
                 nc.scalar.copy(
                     out=sums[(k, flat // SW)][:, flat % SW : flat % SW + step],
@@ -173,7 +176,12 @@ def tile_routed_moe_kernel(tc, xT, w, offs, out):
                 if k == n_units - 1:
                     nc.sync.dma_start(out[b * P : (b + 1) * P, :], windows[b][:])
 
-        for k in range(n_units - 2):
+        def send_back0(b):
+            copy = nc.vector.tensor_copy if b == 0 else nc.scalar.copy
+            copy(out=sums[(0, 0)][:, b * C : (b + 1) * C], in_=acc0[b][:, 0:C])
+            scatter(0, b)
+
+        for k in WORDS:
             gather_words(k)
         gather_raw(0, 2)
         gather_raw(0, 3)
@@ -188,23 +196,35 @@ def tile_routed_moe_kernel(tc, xT, w, offs, out):
             for b in range(n0 // P, n1 // P):
                 multiply(0, 0, b, acc0[b][:, 0:C])
             for b in range(n0 // P, n1 // P):
-                copy = nc.vector.tensor_copy if b == 0 else nc.scalar.copy
-                copy(out=sums[(0, 0)][:, b * C : (b + 1) * C], in_=acc0[b][:, 0:C])
-                scatter(0, b)
+                if b < 3 or not LATE0:
+                    send_back0(b)
         for j, c0, c1, copy in CASTS:
             engine = nc.vector.tensor_copy if copy == "vector" else nc.scalar.copy
             engine(out=planes[:, j, c0:c1], in_=plane_raw[j][:, c0:c1])
         nc.scalar.copy(out=planes[:, 2:4, LAST:T], in_=raw23[:, :, LAST:T])
 
         gather_planes(1, (2, 3))
-        prepare(1)
+        open_banks(1)
+        weights(1, 0, 256)
+        if LATE0:
+            send_back0(3)
+        weights(1, 256, N)
         gather_planes(2, (2, 3))
         for k in range(1, n_units):
-            send_back(k, (0, 1))
+            for b in range(SPLIT):
+                send_back(k, (b,))
             if k + 1 == n_units - 1:
                 gather_late(k + 1)
             if k + 1 < n_units:
-                prepare(k + 1)
-            send_back(k, (2, 3))
+                open_banks(k + 1)
+                weights(k + 1, 0, N // 2)
+            for b in range(SPLIT, NB):
+                send_back(k, (b,))
+            if k + 1 < n_units:
+                weights(k + 1, N // 2, N)
             if k + 2 < n_units - 1:
                 gather_late(k + 2)
+            if k in (1, 2):
+                x_grouped[k + 3] = keep.tile([P, 4 * widths[k + 3]], BF16, name="xg_%d" % (k + 3), tag="xg_%d" % k, align_bytes=64)
+            for unit, j in EXTRA.get(k, ()):
+                gather_planes(unit, (j,))

@@ -15,18 +15,16 @@ COPY = mybir.ActivationFunctionType.Copy
 
 P = 128
 NB = N // P
-PIECES = ((0, 1024), (1024, 1536), (1536, 2048))
+PIECES = ((0, 1024), (1024, 2048))
 LAST = 1792
-CASTS = ((2, 0, 1024, "scalar"), (2, 1024, LAST, "scalar"), (3, 0, 512, "vector"), (3, 512, 1024, "vector"), (3, 1024, LAST, "scalar"))
+CASTS = ((2, 0, LAST, "scalar"), (3, 0, LAST, "scalar"))
 BANK = 512
-SW = 1024
-UNITS = ((0, 1), (1, 1), (2, 1), (3, 1), (4, 2), (6, 2))
-WORDS = (0, 1, 2, 3)
-EXTRA = {1: ((4, 0), (4, 1)), 2: ((5, 0),), 3: ((5, 1),)}
-LATE0 = True
-SPLIT = 2
-VIL = ((1, 0),)
+UNITS = ((0, 1), (1, 1), (2, 2), (4, 2), (6, 2))
+EARLY = 3
 W0_CUTS = (0, 128, 256, 512)
+HALF = N // 2
+SPLIT = {1: 3, 2: 3, 3: 3, 4: 2}
+GPOS = {1: 3, 2: 3, 3: 3}
 
 
 def tile_routed_moe_kernel(tc, xT, w, offs, out):
@@ -36,7 +34,7 @@ def tile_routed_moe_kernel(tc, xT, w, offs, out):
         stage = ctx.enter_context(tc.tile_pool(name="stage", bufs=3))
         sums_pool = ctx.enter_context(tc.tile_pool(name="sums", bufs=4))
         wstage = ctx.enter_context(tc.tile_pool(name="wstage", bufs=8))
-        wint = ctx.enter_context(tc.tile_pool(name="wint", bufs=4))
+        wint = ctx.enter_context(tc.tile_pool(name="wint", bufs=2))
         psum = ctx.enter_context(tc.psum_pool(name="psum", bufs=8))
 
         x_view = xT.rearrange("(p j) t -> p j t", j=4)
@@ -59,40 +57,46 @@ def tile_routed_moe_kernel(tc, xT, w, offs, out):
         nc.sync.dma_start(plane_raw[3], x_view[:, 3, :])
         for n0, n1 in zip(W0_CUTS[1:-1], W0_CUTS[2:]):
             load_w(0, n0, n1)
-        for e in range(1, E):
+        load_w(1, 0, HALF)
+        load_w(1, HALF, N)
+        for e in range(2, E):
             load_w(e, 0, N)
 
         pairs = keep.tile([P, T, 2], BF16, name="xpairs")
         planes = keep.tile([P, 4, T], BF16, name="xplanes")
         for (c0, c1), piece in zip(PIECES, pair_raw):
             nc.vector.tensor_copy(out=pairs[:, c0:c1, :], in_=piece[:].rearrange("p e t -> p t e"))
+        for (c0, c1), piece in zip(PIECES, pair_raw):
             nc.scalar.copy(out=planes[:, 0:2, c0:c1], in_=piece[:])
 
         widths = [n * C for (first, n) in UNITS]
         starts = [first * C for (first, n) in UNITS]
         n_units = len(UNITS)
-        x_grouped = {}
-        for k in range(n_units - 2):
-            x_grouped[k] = keep.tile([P, 4 * widths[k]], BF16, name="xg_%d" % k, tag="xg_%d" % k, align_bytes=64)
+        early_slots = sum(widths[:EARLY])
+        x_early = keep.tile([P, 4 * early_slots], BF16, name="x_early", tag="xg", align_bytes=64)
+        x_grouped = {k: x_early[:, 4 * starts[k] : 4 * (starts[k] + widths[k])] for k in range(EARLY)}
         x_codes = [keep.tile([P, widths[k]], U32, name="xc_%d" % k, align_bytes=64) for k in range(n_units)]
         x_scales = [keep.tile([P, widths[k]], U8, name="xs_%d" % k, align_bytes=64) for k in range(n_units)]
-        sums = {}
         windows = [keep.tile([P, T], F32, name="window_%d" % b) for b in range(NB)]
         w_codes = {}
         w_scales = {}
         banks = {}
+        sums = {}
+
+        def list_slice(first, n):
+            return offsets[:, first // 16 : (first + n) // 16]
 
         def unit_offsets(k):
-            return offsets[:, starts[k] // 16 : (starts[k] + widths[k]) // 16]
+            return list_slice(starts[k], widths[k])
 
         def slot_planes(k):
-            return x_grouped[k][:].rearrange("p (s j) -> p s j", j=4)
+            return x_grouped[k].rearrange("p (s j) -> p s j", j=4)
 
-        def gather_words(k):
+        def gather_words(target, first, n):
             table = pairs[:].rearrange("p t e -> p (t e)").bitcast(U32)
             nc.vector.tensor_copy(
-                out=x_grouped[k][:].bitcast(U32).rearrange("p (s u) -> p s u", u=2)[:, :, 0],
-                in_=table.indirect(unit_offsets(k)),
+                out=target.bitcast(U32).rearrange("p (s u) -> p s u", u=2)[:, :, 0],
+                in_=table.indirect(list_slice(first, n)),
             )
 
         def gather_raw(k, j):
@@ -104,29 +108,39 @@ def tile_routed_moe_kernel(tc, xT, w, offs, out):
                     out=slot_planes(k)[:, :, j], in_=planes[:, j, :].indirect(unit_offsets(k)), func=COPY
                 )
 
-        def gather_late(k):
-            gather_planes(k, (2, 3))
+        def open_late(k):
+            late = keep.tile([P, 4 * widths[k]], BF16, name="xg_%d" % k, tag="xg", align_bytes=64)
+            x_grouped[k] = late[:]
+
+        def gather_next(k):
+            if k >= EARLY:
+                open_late(k)
+            gather_planes(k, (2, 3) if k < EARLY else (0, 1, 2, 3))
 
         def quantize_x(k):
-            nc.vector.quantize_mx(out=x_codes[k][:].bitcast(FP8X4), scales=x_scales[k][:], in_=x_grouped[k][:])
+            nc.vector.quantize_mx(out=x_codes[k][:].bitcast(FP8X4), scales=x_scales[k][:], in_=x_grouped[k])
 
-        def interleave(e, n0, n1, copy):
-            grouped = wint.tile([P, n1 - n0, 4], BF16, align_bytes=64)
-            copy(
-                out=grouped[:].rearrange("p (c i) j -> p c j i", i=4),
-                in_=w_raw[e][:, :, n0:n1].rearrange("p j (c i) -> p c j i", i=4),
-            )
-            return grouped
+        def quantize_w(experts, n0, n1, copy):
+            cols = n1 - n0
+            grouped = wint.tile([P, len(experts), cols, 4], BF16, align_bytes=64)
+            for i, e in enumerate(experts):
+                copy(
+                    out=grouped[:, i, :, :].rearrange("p (c i) j -> p c j i", i=4),
+                    in_=w_raw[e][:, :, n0:n1].rearrange("p j (c i) -> p c j i", i=4),
+                )
+            codes = keep.tile([P, len(experts) * cols], U32, name="wc_%d_%d" % (experts[0], n0), align_bytes=64)
+            scales = keep.tile([P, len(experts) * cols], U8, name="ws_%d_%d" % (experts[0], n0), align_bytes=64)
+            return grouped, codes, scales
 
-        def quantize_w(e, n0, n1, grouped):
-            codes = keep.tile([P, n1 - n0], U32, name="wc_%d_%d" % (e, n0), align_bytes=64)
-            scales = keep.tile([P, n1 - n0], U8, name="ws_%d_%d" % (e, n0), align_bytes=64)
+        def finish_w(experts, n0, n1, grouped, codes, scales):
             nc.vector.quantize_mx(
-                out=codes[:].bitcast(FP8X4), scales=scales[:], in_=grouped[:].rearrange("p n j -> p (n j)")
+                out=codes[:].bitcast(FP8X4), scales=scales[:], in_=grouped[:].rearrange("p e n j -> p (e n j)")
             )
-            for b in range(n0 // P, n1 // P):
-                w_codes[(e, b)] = codes[:, b * P - n0 : (b + 1) * P - n0]
-                w_scales[(e, b)] = scales[:, b * P - n0 : (b + 1) * P - n0]
+            for i, e in enumerate(experts):
+                for b in range(n0 // P, n1 // P):
+                    c0 = i * (n1 - n0) + b * P - n0
+                    w_codes[(e, b)] = codes[:, c0 : c0 + P]
+                    w_scales[(e, b)] = scales[:, c0 : c0 + P]
 
         def multiply(k, e, b, acc):
             s = (e - UNITS[k][0]) * C
@@ -140,91 +154,67 @@ def tile_routed_moe_kernel(tc, xT, w, offs, out):
                 stop=True,
             )
 
-        def scatter(k, b):
-            flat = b * widths[k]
-            nc.vector.tensor_copy(
-                out=windows[b][:].indirect(unit_offsets(k)),
-                in_=sums[(k, flat // SW)][:, flat % SW : flat % SW + widths[k]],
-            )
-
-        def open_banks(k):
-            quantize_x(k)
-            for i in range(NB * widths[k] // BANK):
-                banks[(k, i)] = psum.tile([P, BANK], F32, name="acc", tag="acc")
-
-        def weights(k, n0, n1):
+        def weights(k, n0, n1, parts=None):
             first, n = UNITS[k]
-            for e in range(first, first + n):
-                copy = nc.vector.tensor_copy if (e, n0) in VIL else nc.scalar.copy
-                quantize_w(e, n0, n1, interleave(e, n0, n1, copy))
+            experts = list(range(first, first + n))
+            if parts is None:
+                parts = quantize_w(experts, n0, n1, nc.scalar.copy)
+            finish_w(experts, n0, n1, *parts)
             for b in range(n0 // P, n1 // P):
-                for e in range(first, first + n):
-                    flat = b * widths[k] + (e - first) * C
-                    multiply(k, e, b, banks[(k, flat // BANK)][:, flat % BANK : flat % BANK + C])
+                for e in experts:
+                    flat = (e - first) * C
+                    if (k, b, flat // BANK) not in banks:
+                        banks[(k, b, flat // BANK)] = psum.tile([P, BANK], F32, name="acc", tag="acc")
+                    multiply(k, e, b, banks[(k, b, flat // BANK)][:, flat % BANK : flat % BANK + C])
 
-        def send_back(k, blocks):
+        def send_back(k, b):
+            back = sums_pool.tile([P, widths[k]], F32, name="sums_%d_%d" % (k, b), tag="sums")
             step = min(widths[k], BANK)
-            for flat in range(blocks[0] * widths[k], (blocks[-1] + 1) * widths[k], step):
-                if (k, flat // SW) not in sums:
-                    sums[(k, flat // SW)] = sums_pool.tile([P, SW], F32, name="sums_%d_%d" % (k, flat // SW), tag="sums")
-                nc.scalar.copy(
-                    out=sums[(k, flat // SW)][:, flat % SW : flat % SW + step],
-                    in_=banks[(k, flat // BANK)][:, flat % BANK : flat % BANK + step],
-                )
-            for b in blocks:
-                scatter(k, b)
-                if k == n_units - 1:
-                    nc.sync.dma_start(out[b * P : (b + 1) * P, :], windows[b][:])
+            for flat in range(0, widths[k], step):
+                copy = nc.vector.tensor_copy if k == 0 and b == 0 else nc.scalar.copy
+                copy(out=back[:, flat : flat + step], in_=banks[(k, b, flat // BANK)][:, 0:step])
+            nc.vector.tensor_copy(out=windows[b][:].indirect(unit_offsets(k)), in_=back[:])
+            if k == n_units - 1:
+                nc.sync.dma_start(out[b * P : (b + 1) * P, :], windows[b][:])
 
-        def send_back0(b):
-            copy = nc.vector.tensor_copy if b == 0 else nc.scalar.copy
-            copy(out=sums[(0, 0)][:, b * C : (b + 1) * C], in_=acc0[b][:, 0:C])
-            scatter(0, b)
-
-        for k in WORDS:
-            gather_words(k)
+        gather_words(x_early[:], 0, early_slots)
         gather_raw(0, 2)
         gather_raw(0, 3)
-        sums[(0, 0)] = sums_pool.tile([P, SW], F32, name="sums_0_0", tag="sums")
-        acc0 = [psum.tile([P, BANK], F32, name="acc0_%d" % b, tag="acc") for b in range(NB)]
         for n0, n1 in zip(W0_CUTS[:-1], W0_CUTS[1:]):
             first_cut = n0 == 0
-            grouped = interleave(0, n0, n1, nc.vector.tensor_copy if first_cut else nc.scalar.copy)
+            parts = quantize_w([0], n0, n1, nc.vector.tensor_copy if n1 <= HALF else nc.scalar.copy)
             if first_cut:
                 quantize_x(0)
-            quantize_w(0, n0, n1, grouped)
+            finish_w([0], n0, n1, *parts)
             for b in range(n0 // P, n1 // P):
-                multiply(0, 0, b, acc0[b][:, 0:C])
-            for b in range(n0 // P, n1 // P):
-                if b < 3 or not LATE0:
-                    send_back0(b)
+                banks[(0, b, 0)] = psum.tile([P, BANK], F32, name="acc", tag="acc")
+                multiply(0, 0, b, banks[(0, b, 0)][:, 0:C])
+            if first_cut:
+                send_back(0, 0)
+        send_back(0, 1)
+        send_back(0, 2)
         for j, c0, c1, copy in CASTS:
             engine = nc.vector.tensor_copy if copy == "vector" else nc.scalar.copy
             engine(out=planes[:, j, c0:c1], in_=plane_raw[j][:, c0:c1])
         nc.scalar.copy(out=planes[:, 2:4, LAST:T], in_=raw23[:, :, LAST:T])
 
+        parts = quantize_w([1], 0, HALF, nc.scalar.copy)
         gather_planes(1, (2, 3))
-        open_banks(1)
-        weights(1, 0, 256)
-        if LATE0:
-            send_back0(3)
-        weights(1, 256, N)
-        gather_planes(2, (2, 3))
+        quantize_x(1)
+        weights(1, 0, HALF, parts)
+        send_back(0, 3)
+        weights(1, HALF, N)
         for k in range(1, n_units):
-            for b in range(SPLIT):
-                send_back(k, (b,))
-            if k + 1 == n_units - 1:
-                gather_late(k + 1)
+            for b in range(SPLIT[k]):
+                if b == GPOS.get(k):
+                    gather_next(k + 1)
+                send_back(k, b)
+            if GPOS.get(k) == SPLIT[k]:
+                gather_next(k + 1)
             if k + 1 < n_units:
-                open_banks(k + 1)
-                weights(k + 1, 0, N // 2)
-            for b in range(SPLIT, NB):
-                send_back(k, (b,))
+                quantize_x(k + 1)
+                weights(k + 1, 0, HALF)
+            for b in range(SPLIT[k], NB):
+                send_back(k, b)
             if k + 1 < n_units:
-                weights(k + 1, N // 2, N)
-            if k + 2 < n_units - 1:
-                gather_late(k + 2)
-            if k in (1, 2):
-                x_grouped[k + 3] = keep.tile([P, 4 * widths[k + 3]], BF16, name="xg_%d" % (k + 3), tag="xg_%d" % k, align_bytes=64)
-            for unit, j in EXTRA.get(k, ()):
-                gather_planes(unit, (j,))
+                weights(k + 1, HALF, N)

@@ -15,8 +15,8 @@ COPY = mybir.ActivationFunctionType.Copy
 
 P = 128
 NB = N // P
-PIECES = ((0, 1024), (1024, 2048))
-LAST = 1792
+PIECES = ((0, 1280), (1280, 2048))
+LAST = 1536
 CASTS = ((2, 0, LAST, "scalar"), (3, 0, LAST, "scalar"))
 BANK = 512
 UNITS = ((0, 1), (1, 1), (2, 2), (4, 2), (6, 2))
@@ -52,8 +52,8 @@ def tile_routed_moe_kernel(tc, xT, w, offs, out):
         def load_w(e, n0, n1):
             nc.sync.dma_start(w_raw[e][:, :, n0:n1], w[e].rearrange("(p j) n -> p j n", j=4)[:, :, n0:n1])
 
-        nc.sync.dma_start(plane_raw[2], x_view[:, 2, :])
         load_w(0, W0_CUTS[0], W0_CUTS[1])
+        nc.sync.dma_start(plane_raw[2], x_view[:, 2, :])
         nc.sync.dma_start(plane_raw[3], x_view[:, 3, :])
         for n0, n1 in zip(W0_CUTS[1:-1], W0_CUTS[2:]):
             load_w(0, n0, n1)
@@ -182,7 +182,7 @@ def tile_routed_moe_kernel(tc, xT, w, offs, out):
         gather_raw(0, 3)
         for n0, n1 in zip(W0_CUTS[:-1], W0_CUTS[1:]):
             first_cut = n0 == 0
-            parts = quantize_w([0], n0, n1, nc.vector.tensor_copy if n1 <= HALF else nc.scalar.copy)
+            parts = quantize_w([0], n0, n1, nc.vector.tensor_copy if n0 == 128 else nc.scalar.copy)
             if first_cut:
                 quantize_x(0)
             finish_w([0], n0, n1, *parts)

@@ -73,10 +73,19 @@ def tile_routed_moe_kernel(tc, xT, w, offs, out):
         starts = [first * C for (first, n) in UNITS]
         n_units = len(UNITS)
         early_slots = sum(widths[:EARLY])
+        half_cols = {k: UNITS[k][1] * HALF for k in range(n_units)}
+        joint = range(EARLY, n_units)
         x_early = keep.tile([P, 4 * early_slots], BF16, name="x_early", tag="xg", align_bytes=64)
         x_grouped = {k: x_early[:, 4 * starts[k] : 4 * (starts[k] + widths[k])] for k in range(EARLY)}
-        x_codes = [keep.tile([P, widths[k]], U32, name="xc_%d" % k, align_bytes=64) for k in range(n_units)]
-        x_scales = [keep.tile([P, widths[k]], U8, name="xs_%d" % k, align_bytes=64) for k in range(n_units)]
+        unit_tile = {}
+        x_codes = []
+        x_scales = []
+        for k in range(n_units):
+            cols = widths[k] + (half_cols[k] if k in joint else 0)
+            xc = keep.tile([P, cols], U32, name="xc_%d" % k, align_bytes=64)
+            xs = keep.tile([P, cols], U8, name="xs_%d" % k, align_bytes=64)
+            x_codes.append(xc)
+            x_scales.append(xs)
         windows = [keep.tile([P, T], F32, name="window_%d" % b) for b in range(NB)]
         w_codes = {}
         w_scales = {}
@@ -109,8 +118,9 @@ def tile_routed_moe_kernel(tc, xT, w, offs, out):
                 )
 
         def open_late(k):
-            late = keep.tile([P, 4 * widths[k]], BF16, name="xg_%d" % k, tag="xg", align_bytes=64)
-            x_grouped[k] = late[:]
+            late = keep.tile([P, 4 * (widths[k] + half_cols[k])], BF16, name="xg_%d" % k, tag="xg", align_bytes=64)
+            unit_tile[k] = late[:]
+            x_grouped[k] = late[:, 0 : 4 * widths[k]]
 
         def gather_next(k):
             if k >= EARLY:
@@ -120,25 +130,30 @@ def tile_routed_moe_kernel(tc, xT, w, offs, out):
         def quantize_x(k):
             nc.vector.quantize_mx(out=x_codes[k][:].bitcast(FP8X4), scales=x_scales[k][:], in_=x_grouped[k])
 
-        def quantize_w(experts, n0, n1, copy):
-            cols = n1 - n0
-            grouped = wint.tile([P, len(experts), cols, 4], BF16, align_bytes=64)
+        def interleave(target, experts, n0, n1, copy):
+            cols = 4 * (n1 - n0)
             for i, e in enumerate(experts):
                 copy(
-                    out=grouped[:, i, :, :].rearrange("p (c i) j -> p c j i", i=4),
+                    out=target[:, i * cols : (i + 1) * cols].rearrange("p (c i j) -> p c j i", i=4, j=4),
                     in_=w_raw[e][:, :, n0:n1].rearrange("p j (c i) -> p c j i", i=4),
                 )
+
+        def quantize_w(experts, n0, n1, copy):
+            cols = n1 - n0
+            grouped = wint.tile([P, len(experts) * cols * 4], BF16, align_bytes=64)
+            interleave(grouped[:], experts, n0, n1, copy)
             codes = keep.tile([P, len(experts) * cols], U32, name="wc_%d_%d" % (experts[0], n0), align_bytes=64)
             scales = keep.tile([P, len(experts) * cols], U8, name="ws_%d_%d" % (experts[0], n0), align_bytes=64)
             return grouped, codes, scales
 
         def finish_w(experts, n0, n1, grouped, codes, scales):
-            nc.vector.quantize_mx(
-                out=codes[:].bitcast(FP8X4), scales=scales[:], in_=grouped[:].rearrange("p e n j -> p (e n j)")
-            )
+            nc.vector.quantize_mx(out=codes[:].bitcast(FP8X4), scales=scales[:], in_=grouped[:])
+            name_w(experts, n0, n1, codes, scales, 0)
+
+        def name_w(experts, n0, n1, codes, scales, base):
             for i, e in enumerate(experts):
                 for b in range(n0 // P, n1 // P):
-                    c0 = i * (n1 - n0) + b * P - n0
+                    c0 = base + i * (n1 - n0) + b * P - n0
                     w_codes[(e, b)] = codes[:, c0 : c0 + P]
                     w_scales[(e, b)] = scales[:, c0 : c0 + P]
 
@@ -157,9 +172,14 @@ def tile_routed_moe_kernel(tc, xT, w, offs, out):
         def weights(k, n0, n1, parts=None):
             first, n = UNITS[k]
             experts = list(range(first, first + n))
-            if parts is None:
-                parts = quantize_w(experts, n0, n1, nc.scalar.copy)
-            finish_w(experts, n0, n1, *parts)
+            if n0 == 0 and k in joint:
+                interleave(unit_tile[k][:, 4 * widths[k] :], experts, n0, n1, nc.scalar.copy)
+                nc.vector.quantize_mx(out=x_codes[k][:].bitcast(FP8X4), scales=x_scales[k][:], in_=unit_tile[k])
+                name_w(experts, n0, n1, x_codes[k], x_scales[k], widths[k])
+            else:
+                if parts is None:
+                    parts = quantize_w(experts, n0, n1, nc.scalar.copy)
+                finish_w(experts, n0, n1, *parts)
             for b in range(n0 // P, n1 // P):
                 for e in experts:
                     flat = (e - first) * C
@@ -177,7 +197,7 @@ def tile_routed_moe_kernel(tc, xT, w, offs, out):
             if k == n_units - 1:
                 nc.sync.dma_start(out[b * P : (b + 1) * P, :], windows[b][:])
 
-        gather_words(x_early[:], 0, early_slots)
+        gather_words(x_early[:, 0 : 4 * early_slots], 0, early_slots)
         gather_raw(0, 2)
         gather_raw(0, 3)
         for n0, n1 in zip(W0_CUTS[:-1], W0_CUTS[1:]):
@@ -212,7 +232,8 @@ def tile_routed_moe_kernel(tc, xT, w, offs, out):
             if GPOS.get(k) == SPLIT[k]:
                 gather_next(k + 1)
             if k + 1 < n_units:
-                quantize_x(k + 1)
+                if k + 1 not in joint:
+                    quantize_x(k + 1)
                 weights(k + 1, 0, HALF)
             for b in range(SPLIT[k], NB):
                 send_back(k, b)

from contextlib import ExitStack

import concourse.mybir as mybir

K, T, E, C, N = 512, 2048, 8, 256, 512
FLOPS = 2 * K * N * E * C

F32 = mybir.dt.float32
BF16 = mybir.dt.bfloat16
U32 = mybir.dt.uint32
U16 = mybir.dt.uint16
U8 = mybir.dt.uint8
FP8X4 = mybir.dt.float8_e4m3fn_x4
COPY = mybir.ActivationFunctionType.Copy

P = 128
NB = N // P
PIECES = ((0, 1280), (1280, 2048))
LAST = 1536
CASTS = ((2, 0, LAST, "scalar"), (3, 0, LAST, "scalar"))
BANK = 512
UNITS = ((0, 1), (1, 1), (2, 2), (4, 2), (6, 2))
EARLY = 3
W0_CUTS = (0, 128, 256, 512)
HALF = N // 2
SPLIT = {1: 3, 2: 3, 3: 3, 4: 2}
GPOS = {1: 3, 2: 3, 3: 3}


def tile_routed_moe_kernel(tc, xT, w, offs, out):
    nc = tc.nc
    with ExitStack() as ctx:
        keep = ctx.enter_context(tc.tile_pool(name="keep", bufs=1))
        stage = ctx.enter_context(tc.tile_pool(name="stage", bufs=3))
        sums_pool = ctx.enter_context(tc.tile_pool(name="sums", bufs=4))
        wstage = ctx.enter_context(tc.tile_pool(name="wstage", bufs=8))
        wint = ctx.enter_context(tc.tile_pool(name="wint", bufs=2))
        psum = ctx.enter_context(tc.psum_pool(name="psum", bufs=8))

        x_view = xT.rearrange("(p j) t -> p j t", j=4)
        pair_raw = []
        for c0, c1 in PIECES:
            piece = stage.tile([P, 2, c1 - c0], F32, name="xpair_%d" % c0, tag="stage")
            nc.sync.dma_start(piece[:], x_view[:, 0:2, c0:c1])
            pair_raw.append(piece)
        offsets = keep.tile([P, T // 16], U16, name="offsets")
        nc.sync.dma_start(offsets[:], offs)
        w_raw = [wstage.tile([P, 4, N], F32, name="w_raw_%d" % e, tag="w_raw") for e in range(E)]
        raw23 = keep.tile([P, 2, T], F32, name="raw23")
        plane_raw = {j: raw23[:, j - 2, :] for j in (2, 3)}

        def load_w(e, n0, n1):
            nc.sync.dma_start(w_raw[e][:, :, n0:n1], w[e].rearrange("(p j) n -> p j n", j=4)[:, :, n0:n1])

        load_w(0, W0_CUTS[0], W0_CUTS[1])
        nc.sync.dma_start(plane_raw[2], x_view[:, 2, :])
        nc.sync.dma_start(plane_raw[3], x_view[:, 3, :])
        for n0, n1 in zip(W0_CUTS[1:-1], W0_CUTS[2:]):
            load_w(0, n0, n1)
        load_w(1, 0, HALF)
        load_w(1, HALF, N)
        for e in range(2, E):
            load_w(e, 0, N)

        pairs = keep.tile([P, T, 2], BF16, name="xpairs")
        planes = keep.tile([P, 4, T], BF16, name="xplanes")
        for (c0, c1), piece in zip(PIECES, pair_raw):
            nc.vector.tensor_copy(out=pairs[:, c0:c1, :], in_=piece[:].rearrange("p e t -> p t e"))
        for (c0, c1), piece in zip(PIECES, pair_raw):
            nc.scalar.copy(out=planes[:, 0:2, c0:c1], in_=piece[:])

        widths = [n * C for (first, n) in UNITS]
        starts = [first * C for (first, n) in UNITS]
        n_units = len(UNITS)
        early_slots = sum(widths[:EARLY])
        half_cols = {k: UNITS[k][1] * HALF for k in range(n_units)}
        joint = range(EARLY, n_units)
        x_early = keep.tile([P, 4 * early_slots], BF16, name="x_early", tag="xg", align_bytes=64)
        x_grouped = {k: x_early[:, 4 * starts[k] : 4 * (starts[k] + widths[k])] for k in range(EARLY)}
        unit_tile = {}
        x_codes = []
        x_scales = []
        for k in range(n_units):
            cols = widths[k] + (half_cols[k] if k in joint else 0)
            xc = keep.tile([P, cols], U32, name="xc_%d" % k, align_bytes=64)
            xs = keep.tile([P, cols], U8, name="xs_%d" % k, align_bytes=64)
            x_codes.append(xc)
            x_scales.append(xs)
        windows = [keep.tile([P, T], F32, name="window_%d" % b) for b in range(NB)]
        w_codes = {}
        w_scales = {}
        banks = {}
        sums = {}

        def list_slice(first, n):
            return offsets[:, first // 16 : (first + n) // 16]

        def unit_offsets(k):
            return list_slice(starts[k], widths[k])

        def slot_planes(k):
            return x_grouped[k].rearrange("p (s j) -> p s j", j=4)

        def gather_words(target, first, n):
            table = pairs[:].rearrange("p t e -> p (t e)").bitcast(U32)
            nc.vector.tensor_copy(
                out=target.bitcast(U32).rearrange("p (s u) -> p s u", u=2)[:, :, 0],
                in_=table.indirect(list_slice(first, n)),
            )

        def gather_raw(k, j):
            nc.vector.tensor_copy(out=slot_planes(k)[:, :, j], in_=plane_raw[j].indirect(unit_offsets(k)))

        def gather_planes(k, which):
            for j in which:
                nc.scalar.activation(
                    out=slot_planes(k)[:, :, j], in_=planes[:, j, :].indirect(unit_offsets(k)), func=COPY
                )

        def open_late(k):
            late = keep.tile([P, 4 * (widths[k] + half_cols[k])], BF16, name="xg_%d" % k, tag="xg", align_bytes=64)
            unit_tile[k] = late[:]
            x_grouped[k] = late[:, 0 : 4 * widths[k]]

        def gather_next(k):
            if k >= EARLY:
                open_late(k)
            gather_planes(k, (2, 3) if k < EARLY else (0, 1, 2, 3))

        def quantize_x(k):
            nc.vector.quantize_mx(out=x_codes[k][:].bitcast(FP8X4), scales=x_scales[k][:], in_=x_grouped[k])

        def interleave(target, experts, n0, n1, copy):
            cols = 4 * (n1 - n0)
            for i, e in enumerate(experts):
                copy(
                    out=target[:, i * cols : (i + 1) * cols].rearrange("p (c i j) -> p c j i", i=4, j=4),
                    in_=w_raw[e][:, :, n0:n1].rearrange("p j (c i) -> p c j i", i=4),
                )

        def quantize_w(experts, n0, n1, copy):
            cols = n1 - n0
            grouped = wint.tile([P, len(experts) * cols * 4], BF16, align_bytes=64)
            interleave(grouped[:], experts, n0, n1, copy)
            codes = keep.tile([P, len(experts) * cols], U32, name="wc_%d_%d" % (experts[0], n0), align_bytes=64)
            scales = keep.tile([P, len(experts) * cols], U8, name="ws_%d_%d" % (experts[0], n0), align_bytes=64)
            return grouped, codes, scales

        def finish_w(experts, n0, n1, grouped, codes, scales):
            nc.vector.quantize_mx(out=codes[:].bitcast(FP8X4), scales=scales[:], in_=grouped[:])
            name_w(experts, n0, n1, codes, scales, 0)

        def name_w(experts, n0, n1, codes, scales, base):
            for i, e in enumerate(experts):
                for b in range(n0 // P, n1 // P):
                    c0 = base + i * (n1 - n0) + b * P - n0
                    w_codes[(e, b)] = codes[:, c0 : c0 + P]
                    w_scales[(e, b)] = scales[:, c0 : c0 + P]

        def multiply(k, e, b, acc):
            s = (e - UNITS[k][0]) * C
            nc.tensor.matmul_mx(
                out=acc,
                lhsT=w_codes[(e, b)].bitcast(FP8X4),
                lhsT_scale=w_scales[(e, b)],
                rhs=x_codes[k][:, s : s + C].bitcast(FP8X4),
                rhs_scale=x_scales[k][:, s : s + C],
                start=True,
                stop=True,
            )

        def weights(k, n0, n1, parts=None):
            first, n = UNITS[k]
            experts = list(range(first, first + n))
            if n0 == 0 and k in joint:
                interleave(unit_tile[k][:, 4 * widths[k] :], experts, n0, n1, nc.scalar.copy)
                nc.vector.quantize_mx(out=x_codes[k][:].bitcast(FP8X4), scales=x_scales[k][:], in_=unit_tile[k])
                name_w(experts, n0, n1, x_codes[k], x_scales[k], widths[k])
            else:
                if parts is None:
                    parts = quantize_w(experts, n0, n1, nc.scalar.copy)
                finish_w(experts, n0, n1, *parts)
            for b in range(n0 // P, n1 // P):
                for e in experts:
                    flat = (e - first) * C
                    if (k, b, flat // BANK) not in banks:
                        banks[(k, b, flat // BANK)] = psum.tile([P, BANK], F32, name="acc", tag="acc")
                    multiply(k, e, b, banks[(k, b, flat // BANK)][:, flat % BANK : flat % BANK + C])

        def send_back(k, b):
            back = sums_pool.tile([P, widths[k]], F32, name="sums_%d_%d" % (k, b), tag="sums")
            step = min(widths[k], BANK)
            for flat in range(0, widths[k], step):
                copy = nc.vector.tensor_copy if k == 0 and b == 0 else nc.scalar.copy
                copy(out=back[:, flat : flat + step], in_=banks[(k, b, flat // BANK)][:, 0:step])
            nc.vector.tensor_copy(out=windows[b][:].indirect(unit_offsets(k)), in_=back[:])
            if k == n_units - 1:
                nc.sync.dma_start(out[b * P : (b + 1) * P, :], windows[b][:])

        gather_words(x_early[:, 0 : 4 * early_slots], 0, early_slots)
        gather_raw(0, 2)
        gather_raw(0, 3)
        for n0, n1 in zip(W0_CUTS[:-1], W0_CUTS[1:]):
            first_cut = n0 == 0
            parts = quantize_w([0], n0, n1, nc.vector.tensor_copy if n0 == 128 else nc.scalar.copy)
            if first_cut:
                quantize_x(0)
            finish_w([0], n0, n1, *parts)
            for b in range(n0 // P, n1 // P):
                banks[(0, b, 0)] = psum.tile([P, BANK], F32, name="acc", tag="acc")
                multiply(0, 0, b, banks[(0, b, 0)][:, 0:C])
            if first_cut:
                send_back(0, 0)
        send_back(0, 1)
        send_back(0, 2)
        for j, c0, c1, copy in CASTS:
            engine = nc.vector.tensor_copy if copy == "vector" else nc.scalar.copy
            engine(out=planes[:, j, c0:c1], in_=plane_raw[j][:, c0:c1])
        nc.scalar.copy(out=planes[:, 2:4, LAST:T], in_=raw23[:, :, LAST:T])

        parts = quantize_w([1], 0, HALF, nc.scalar.copy)
        gather_planes(1, (2, 3))
        quantize_x(1)
        weights(1, 0, HALF, parts)
        send_back(0, 3)
        weights(1, HALF, N)
        for k in range(1, n_units):
            for b in range(SPLIT[k]):
                if b == GPOS.get(k):
                    gather_next(k + 1)
                send_back(k, b)
            if GPOS.get(k) == SPLIT[k]:
                gather_next(k + 1)
            if k + 1 < n_units:
                if k + 1 not in joint:
                    quantize_x(k + 1)
                weights(k + 1, 0, HALF)
            for b in range(SPLIT[k], NB):
                send_back(k, b)
            if k + 1 < n_units:
                weights(k + 1, HALF, N)
